import numpy as np, ml_dtypes
CORES = [48,51,52,55]
N = 4
BF = ml_dtypes.bfloat16
W, C, M, V, D, Q = 4096, 256, 3, 5, 1, 9
LM = 127
def parts(rng):
    return (rng.integers(0, 256, (N, 8, 16, W)), rng.integers(0, W, (N, 8, 16, C)), rng.integers(0, 256, (N, 8, 16, C)),
            rng.integers(0, 16, (N, 8, 16, 1)), rng.integers(48, 81, (N, 8, 16, 1)))
def pack(x, f, z, w, lm):
    return {"rock": x.reshape(N, 128, W).astype(np.float32).astype(BF), "front": np.ascontiguousarray(f.reshape(N, 128, C)).astype(np.int32),
            "vein": z.reshape(N, 128, C).astype(np.float32).astype(BF), "w": w.reshape(N, 128, 1).astype(np.int32), "lim": lm.reshape(N, 128, 1).astype(np.int32)}
def setup_inputs(rng):
    return pack(*parts(rng))
def setup_inputs_alike(rng):
    x, f, z, w, lm = parts(rng); lm = rng.integers(10, 41, (N, 8, 16, 1)); rec = rng.integers(100, 156, (N, 8, 16, 4))
    x = np.take_along_axis(rec, rng.integers(0, 4, (N, 8, 1, W)), 3)
    far = lm + rng.choice(np.array([-1, 0, 0, 0, 1, 2, 3, 4]), (N, 8, 16, C))
    z = np.take_along_axis(rec, rng.integers(0, 4, (N, 8, 1, C)), 3) + rng.choice(np.array([-1, 1]), (N, 8, 16, C)) * far
    f[:, ::2] = rng.choice(np.array([0, W - 1, W // 2, 3]), (N, 4, 16, C))
    f[:, 1] = f[:, 1][..., rng.integers(0, 4, C)]
    return pack(x, f, z, w, lm)
def setup_inputs_corners(rng):
    x, f, z, w, lm = parts(rng); end = np.array([0, 1, 14, 15]); P = C // 2; h = np.arange(P)
    for a in range(N):
        o = [int(b) for b in rng.permutation(8)]
        for g in range(8):
            v = o[g]
            if v == 0:
                lm[a, g] = 0; w[a, g] = 0
            elif v == 1:
                lm[a, g] = LM; w[a, g] = 15
            elif v in (2, 3, 4):
                x[a, g] = rng.integers(200, 256, (16, W)); z[a, g] = rng.integers(0, 61, (16, C)); lm[a, g] = rng.integers(0, 101, (16, 1))
                s = np.arange(16)[:, None] * (W // 32) + rng.integers(0, W // 32, (16, P)); j = rng.integers(W // 2, W, (16, P))
                if v == 2:
                    k = rng.choice(end, P); l = rng.choice(end, P); k[:16] = np.repeat(end, 4); l[:16] = np.tile(end, 4)
                    s[np.maximum(l, rng.integers(0, 16, P)), h] = s[l, h]
                    j[k, h] = (s[l, h] & -8) + rng.integers(0, 8, P)
                    j[np.maximum(k, rng.integers(0, 16, P)), h] = j[k, h]
                if v == 4:
                    s[:] = W - 1; j[:] = W - 1; s[:, :P // 2] = 0; j[:, :P // 2] = 0
                    s[1:, P // 2:3 * P // 4] = W - 21; j[1:, P // 2:3 * P // 4] = W - 3
                f[a, g][:, 0::2] = s; f[a, g][:, 1::2] = j
            elif v == 5:
                r = rng.integers(64, 192, (16, 1)); x[a, g] = r; lm[a, g] = 0
                off = np.argsort(rng.random((16, C)), axis=0) >= rng.integers(Q - 2, Q + 2, C)[None, :]
                z[a, g] = r + np.where(off, rng.choice(np.array([-40, -4, 4, 40]), (16, C)), 0)
            elif v == 6:
                f[a, g] = (W - 1) * rng.integers(0, 2, (16, C)); w[a, g] = 15 * rng.integers(0, 2, (16, 1)); lm[a, g] = LM * rng.integers(0, 2, (16, 1))
            else:
                w[a, g, 0] = 15; w[a, g, 1] = 1; z[a, g][:, ::2] = 0; z[a, g, 0, ::2] = 136; z[a, g, 1, ::2] = 7; f[a, g][:, ::4] = W - 1
                for i, n, u, m in ((2, W - 3, 2037, 0), (6, W - 15, 2039, 2)):
                    z[a, g, 0, i::8] = 135; z[a, g, 1, i::8] = u - 2025; f[a, g][:, i::8] = n
                    x[a, g][:, (((n * (2 * u + 1)) >> (5 + m)) + n + 613 * m + 37 * np.arange(16)) & (W - 1)] = z[a, g][:, i][:, None]
    return pack(x, f, z, w, lm)
def setup_inputs_ends(rng):
    x, f, z, w, lm = parts(rng)
    x = 255 * np.where(rng.random((N, 8, 1, W)) < 0.4, rng.integers(0, 2, (N, 8, 1, W)), rng.integers(0, 2, (N, 8, 16, W)))
    z = 255 * np.where(rng.random((N, 8, 1, C)) < 0.4, rng.integers(0, 2, (N, 8, 1, C)), rng.integers(0, 2, (N, 8, 16, C)))
    f = (W - 1) * rng.integers(0, 2, f.shape); w = 15 * rng.integers(0, 2, w.shape); lm = LM * rng.integers(0, 2, lm.shape)
    for a, g in ((N - 1, 7), (0, 0)):
        w[a, g] = 15; z[a, g][:, [0, C - 2, C - 1]] = 255; z[a, g][:, [3, C - 3]] = 0
        z[a, g][:, [5, C - 4]] = rng.permutation(np.array([255] * 9 + [26] + [0] * 6))[:, None]
        f[a, g, 15][[0, 3, 5, C - 4, C - 3, C - 2, C - 1]] = W - 1
        for u in ((16 * 15 * 255) & 2047, 0):
            x[a, g][:, ((((W - 1) * (2 * u + 1)) >> (5 + np.arange(M))) + W - 1 + 613 * np.arange(M) + 37 * 15) & (W - 1)] = 0
    return pack(x, f, z, w, lm)
def setup_inputs_full(rng):
    x, f, z, w, lm = parts(rng); P = C // 2; h = np.arange(P); n = W // C
    b = int(rng.integers(0, N)); g = int(rng.integers(0, 8)); rest = [q for q in range(N) if q not in (b, (b - D) % N)]; a = rest[int(rng.integers(0, len(rest)))]
    for q in range(N):
        if q != a:
            x[q, g] = rng.integers(200, 256, (16, W)); z[q, g] = rng.integers(0, 61, (16, C)); lm[q, g] = 0
            f[q, g] = n * rng.permutation(C)[None, :] + rng.integers(0, n, (16, C))
    i = np.array([P - 1, 0, P // 2])[:int(rng.integers(1, 4))]
    f[b, g, 15, 2 * i + 1] = (f[b, g, rng.integers(0, 16, len(i)), 2 * i] & -8) + rng.integers(0, 8, len(i))
    x[a] = rng.integers(200, 256, (8, 16, W)); z[a] = rng.integers(0, 61, (8, 16, C)); lm[a] = rng.integers(80, 121, (8, 16, 1))
    k = rng.integers(0, 16, (8, P)); l = rng.integers(0, 16, (8, P)); gr = np.arange(8)[:, None]; fa = f[a]
    fa[gr, k, 2 * h + 1] = (fa[gr, l, 2 * h] & -8) + rng.integers(0, 8, (8, P))
    o = [int(c) for c in rng.permutation(8)]
    f[a, o[0]] = 0; w[a, o[0]] = 0
    f[a, o[1]] = W - 1; w[a, o[1]] = 0; w[a, o[1], 0] = W >> 9; z[a, o[1], 0] = 32
    return pack(x, f, z, w, lm)
def setup_inputs_spread(rng):
    x = np.minimum((np.exp2(8 * rng.random((N, 8, 1, W))) * rng.random((N, 8, 16, W))).astype(np.int64), 255)
    z = np.minimum((np.exp2(8 * rng.random((N, 8, 1, C))) * rng.random((N, 8, 16, C))).astype(np.int64), 255)
    f = np.minimum((W * rng.random((N, 8, 16, C)) ** 3).astype(np.int64), W - 1)
    return pack(x, f, z, rng.integers(0, 16, (N, 8, 16, 1)), np.minimum((128 * rng.random((N, 8, 16, 1)) ** 2).astype(np.int64), LM))
def check_inputs(d):
    bad = []
    for k, hi in (("rock", 255), ("front", W - 1), ("vein", 255), ("w", 15), ("lim", LM)):
        v = np.asarray(d[k]).astype(np.float64)
        if not (np.min(v) >= 0 and np.max(v) <= hi): bad.append("range of " + k)
        elif np.any(v != np.floor(v)): bad.append("whole numbers in " + k)
    return bad
def reference(rock, front, vein, w, lim):
    x = rock.astype(np.float32).astype(np.int64).reshape(N, 8, 16, W)
    f = front.astype(np.int64).reshape(N, 8, 16, C)
    z = vein.astype(np.float32).astype(np.int64).reshape(N, 8, 16, C)
    wt = w.astype(np.int64).reshape(N, 8, 16, 1); lm = lim.astype(np.int64).reshape(N, 8, 16, 1)
    place = np.arange(16)[:, None]; ci = np.arange(C); met = np.zeros(N, np.int64)
    for t in range(V):
        if t > 0:
            f = np.roll(f, D, axis=0); z = np.roll(z, D, axis=0)
        u = np.add.reduce(wt * z, axis=2) & 2047
        dig = np.add.reduce(z, axis=2) & 15
        top = (lm + (met & 3)[:, None, None, None])[..., None]
        for m in range(M):
            c = (((f * (2 * u[:, :, None, :] + 1)) >> (5 + m)) + f + 613 * m + 37 * place) & (W - 1)
            v = np.take_along_axis(x, c.reshape(N, 8, 1, 16 * C), 3).reshape(N, 8, 16, 16, C)
            dif = np.abs(v - z[:, :, :, None, :])
            score = np.add.reduce(dif, axis=2); near = np.count_nonzero(dif <= top, axis=2)
            if m == 0:
                bs, bc, bn = score, c, near
            else:
                less = score < bs; bs = np.where(less, score, bs); bc = np.where(less, c, bc); bn = np.where(less, near, bn)
        f = np.where(bn >= Q, bc, f)
        sen = ci[((ci >> t) & 1) == 0]; jun = sen + (1 << t)
        fs = f[..., sen]; fj = f[..., jun]
        eq = ((fj[:, :, :, None, :] >> 3) == (fs[:, :, None, :, :] >> 3)).reshape(N, 8, 256, C // 2)
        meet = np.any(eq, axis=2)[:, :, None, :]; first = np.argmax(eq, axis=2)[:, :, None, :]
        k = first >> 4; l = first & 15
        met = np.count_nonzero(meet, axis=(1, 2, 3))
        src = place - l + k
        ns = np.where(meet & (place > l) & (src <= 15), np.take_along_axis(fj, np.minimum(np.maximum(src, 0), 15), 2), fs)
        nj = np.where(meet & (place >= k), (((fj * fs) >> 5) + fj + u[..., jun][:, :, None, :]) & (W - 1), fj)
        f = f.copy(); f[..., sen] = ns; f[..., jun] = nj
        e = np.take_along_axis(f, dig[:, :, None, :], 2)
        old = np.take_along_axis(x, e, 3)
        lo = np.full((N, 8, W), C)
        np.minimum.at(lo, (np.arange(N)[:, None, None], np.arange(8)[None, :, None], e[:, :, 0]), np.broadcast_to(ci, (N, 8, C)))
        zl = np.take_along_axis(z, np.minimum(lo, C - 1)[:, :, None, :], 3)
        x = np.where((lo < C)[:, :, None, :], np.maximum(x - (zl >> 2), 0), x)
        z = (z + old) >> 1
    return {"yx": x.reshape(N, 128, W).astype(np.float32).astype(BF), "yf": f.reshape(N, 128, C).astype(np.float32), "yz": z.reshape(N, 128, C).astype(np.float32).astype(BF)}

import comms_topo
from concourse.mybir import AluOpType as A, AxisListType, ActivationFunctionType as F

W, C, V, Q = 4096, 256, 5, 9
H = 128
TRASH = W
VPART = [64, 64, 64]

SCRATCH = {}
BUF = {}
PLACE = {}
POOL = {"bfloat16": ["PoolB", 0], "float16": ["PoolH", 0], "float32": ["PoolF", 0], "int32": ["PoolI", 0], "uint16": ["PoolU", 0]}
SEMAPHORES = ["cV", "cS", "cP", "cG", "loc"]


def _sb(name, cols, dt):
    BUF[name] = ("sbuf", [128] + (cols if isinstance(cols, list) else [cols]), dt)
    if isinstance(cols, list):
        SCRATCH[name] = BUF[name]
        return
    step = 8 if dt in ("float32", "int32") else 16
    p = POOL[dt]
    PLACE[name] = (p[0], p[1])
    p[1] += (cols + step - 1) // step * step
    SCRATCH[p[0]] = ("sbuf", [128, p[1]], dt)


def _declare():
    b, h, f, i, u = "bfloat16", "float16", "float32", "int32", "uint16"
    _sb("X", W + C, b)
    _sb("vein0", C, b); _sb("front0", C, i); _sb("w0", 1, i); _sb("lim0", 1, i)
    _sb("PI", 1, i); _sb("CI", 128, i); _sb("C15", 128, i); _sb("CG", 128, i)
    _sb("ci", 32, i)
    _sb("cf", 64, f)
    _sb("OHK", 16, f)
    for n in ("BDb", "Ib", "NIb", "W2", "S256", "LT", "LT0", "KBD", "BD64", "BD0"):
        _sb(n, 128, b)
    _sb("IND", 8, b); _sb("IND128", 8, b); _sb("HC", 64, b); _sb("RB", 64, b)
    _sb("BDh", 128, h); _sb("NIh", 128, h); _sb("WI", 160, h); _sb("WC", 160, i)
    _sb("BL", 16 * 128, h); _sb("PW", 8 * 128, b)
    _sb("RM", 7 * 128, h); _sb("CC", 7 * 8, h); _sb("PM", 5 * 128, h)
    _sb("REP", 16 * H, b); _sb("REPI", 16 * H, i)
    _sb("SC0", 64, b); _sb("TRI", [8, 16], b); _sb("ONE", 128, f)
    _sb("TRC", 16, f); _sb("TRI0", 16, i)
    for k in range(2):
        s = str(k)
        for t in range(V):
            _sb("Z%d%d" % (t, k), H, b); _sb("TB%d%d" % (t, k), 4 * H, h)
        for t in range(V - 1):
            _sb("SN%d%d" % (t, k), H, h); _sb("SZ%d%d" % (t, k), H, b)
        _sb("VI" + s, 2 * H, i); _sb("VS" + s, 2 * H, i); _sb("MS" + s, H, b); _sb("NK" + s, 3 * H, f)
        _sb("QI" + s, 3 * H, i); _sb("QS" + s, 3 * H, i); _sb("OF" + s, 3 * H, u); _sb("ZR" + s, 16 * H, b); _sb("ZT" + s, H, b); _sb("NZT" + s, H, b)
        _sb("U32" + s, 64, f); _sb("ZQ" + s, H, h)
        _sb("K0" + s, H, f); _sb("K1" + s, H, f); _sb("KI" + s, H, i); _sb("YI" + s, H, i); _sb("OK" + s, H, i)
        _sb("MK" + s, 4 * H, b); _sb("PR" + s, 4 * H, h)
        _sb("GS" + s, 64, h); _sb("JR" + s, 256, h); _sb("NF" + s, H, f); _sb("FC" + s, H, h); _sb("EQ" + s, 1024, b)
        _sb("M12" + s, H, b); _sb("OH" + s, 64, b); _sb("MM" + s, H, b); _sb("P12" + s, H, b); _sb("TP" + s, 64, b)
        _sb("MS1" + s, 64, b); _sb("MS2" + s, 64, b)
        _sb("DM" + s, 64, f); _sb("DS" + s, 64, f); _sb("DO" + s, 4, u); _sb("TAB" + s, 2048, f)
        _sb("J32" + s, 64, f); _sb("JQ" + s, 64, i); _sb("JT" + s, 64, i); _sb("NEW" + s, H, f)
        _sb("PA" + s, H, h); _sb("PB" + s, H, h); _sb("CNT" + s, 1, f)
        _sb("FS" + s, H, h); _sb("ETF" + s, H, h); _sb("EMP" + s, H, h); _sb("EMN" + s, H, h); _sb("EC" + s, H, h)
        _sb("EPF" + s, 8, f); _sb("YO" + s, 8, u); _sb("ECL" + s, 8, f); _sb("YB" + s, H, b); _sb("ZH" + s, H, h)
        _sb("ED" + s, [8, H], b); _sb("FLG" + s, H, b); _sb("DTM" + s, H, h); _sb("T1" + s, 8, f); _sb("T2" + s, 8, f)
        _sb("SO" + s, 8, u); _sb("NX" + s, H, b)
    _sb("EX", [8, H], b)
    _sb("EI", 2, i); _sb("TOP", 1, f); _sb("YF", C, f); _sb("YZ", C, b)
    for k in range(3):
        _sb("D%d" % k, 16 * H, b); _sb("G%d" % k, 16 * H, b); _sb("L%d" % k, 16 * H, b)
    for k in range(8):
        SCRATCH["B%d" % k] = BUF["B%d" % k] = ("psum", [128, 512], "float32")
    for t in range(1, V):
        for k in range(2):
            SEMAPHORES.append("an%d%d" % (t, k)); SEMAPHORES.append("az%d%d" % (t, k))
    for k in range(20):
        SEMAPHORES.append("d%d" % k)


_declare()

CY = 0.00083
FIX = {"V": 0.06, "S": 0.10, "P": 0.03, "G": 0.15, "Y": 0.1, "A": 0.1}
LAT = 0.08


class _Nothing:
    pass


def _graph():
    return {"ops": [], "acc": {}, "bank": {}}


def _add(gr, q, cost, fn, R, Wr, sem=None):
    ops = gr["ops"]; n = len(ops); deps = set()
    for w, regs in ((False, R), (True, Wr)):
        for (name, a, b) in regs:
            if BUF.get(name, ("",))[0] == "psum":
                ep = gr["bank"].setdefault(name, [None, [], []])
                if ep[0] != q:
                    ep[2] = ep[1]; ep[1] = []; ep[0] = q
                for o in ep[2]:
                    deps.add(o[0])
                for o in ep[1]:
                    if o[1] < b and a < o[2] and (w or o[3]):
                        deps.add(o[0])
                ep[1].append((n, a, b, w))
            else:
                lst = gr["acc"].setdefault(name, [])
                keep = []
                for o in lst:
                    if o[1] < b and a < o[2] and (w or o[3]):
                        deps.add(o[0])
                        if w and a <= o[1] and o[2] <= b and o[0] != n:
                            continue
                    keep.append(o)
                keep.append((n, a, b, w))
                gr["acc"][name] = keep
    deps.discard(n)
    ops.append({"q": q, "cost": cost, "fn": fn, "deps": sorted(deps), "sem": sem})
    return n


def _order(ops):
    n = len(ops); succ = [[] for _ in ops]; need = [0] * n
    for i, o in enumerate(ops):
        need[i] = len(o["deps"])
        for d in o["deps"]:
            succ[d].append(i)
    pr = [0.0] * n
    for i in range(n - 1, -1, -1):
        pr[i] = ops[i]["cost"] + max([pr[s] + LAT for s in succ[i]] or [0.0])
    free = {}; fin = [0.0] * n; est = [0.0] * n; out = []
    ready = {}
    for i in range(n):
        if need[i] == 0:
            ready.setdefault(ops[i]["q"], []).append(i)
    while any(ready.values()):
        best = None
        for q, lst in ready.items():
            if not lst:
                continue
            f = free.get(q, 0.0)
            t0 = min(max(f, est[i]) for i in lst)
            c = max((i for i in lst if max(f, est[i]) <= t0 + 0.04), key=lambda i: pr[i])
            st = max(f, est[c])
            if best is None or st < best[0]:
                best = (st, c, q)
        st, c, q = best
        ready[q].remove(c)
        dur = ops[c]["cost"]
        hold = dur
        if ops[c]["sem"] is not None:
            hold = FIX.get(q, 0.1)
        free[q] = st + hold if q != "A" else 0.0
        fin[c] = st + dur
        ops[c]["start"] = st; ops[c]["fin"] = fin[c]
        out.append(c)
        for s in succ[c]:
            need[s] -= 1
            est[s] = max(est[s], fin[c] + LAT)
            if need[s] == 0:
                ready.setdefault(ops[s]["q"], []).append(s)
    return out


def rank_program(g, core, T, topo):
    rank = T.rank_of(core)
    if rank is None:
        return
    nxt = T.cores[(rank + 1) % len(T.cores)]
    gr = _graph()
    vec, sca, ten, syn = g.vector, g.scalar, g.tensor, g.sync

    def sl(n, a=0, b=None, st=None):
        p, o = PLACE.get(n, (n, 0))
        b = BUF[n][1][1] if b is None else b
        return T[p][:, o + a:o + b:st] if st else T[p][:, o + a:o + b]

    def ap(r):
        return sl(*r)

    def full(n):
        return (n, 0, BUF[n][1][1])

    def reg(r):
        return (r[0], r[1], r[2])

    def cnt(r):
        return (r[2] - r[1] + (r[3] if len(r) > 3 else 1) - 1) // (r[3] if len(r) > 3 else 1)

    def two(*rs):
        return all(BUF[r[0]][2] in ("bfloat16", "float16", "uint16") for r in rs)

    def vc(cy):
        return FIX["V"] + max(64, cy) * CY

    def scal(s):
        return [reg(s)] if isinstance(s, tuple) else []

    def sv(s):
        return ap(s) if isinstance(s, tuple) else s

    def tc(o, i):
        _add(gr, "V", vc(cnt(i) * (0.5 if two(o, i) else 1)), lambda: vec.tensor_copy(out=ap(o), in_=ap(i)), [reg(i)], [reg(o)])

    def ts(o, i, s1, op0, s2=None, op1=None):
        def fn():
            if op1 is None:
                return vec.tensor_scalar(out=ap(o), in0=ap(i), scalar1=sv(s1), scalar2=None, op0=op0)
            return vec.tensor_scalar(out=ap(o), in0=ap(i), scalar1=sv(s1), scalar2=sv(s2), op0=op0, op1=op1)
        _add(gr, "V", vc(cnt(i) * (0.5 if two(o, i) else 1)), fn, [reg(i)] + scal(s1) + scal(s2), [reg(o)])

    def tt(o, i, j, op):
        ps = "psum" in (BUF[i[0]][0], BUF[j[0]][0])
        _add(gr, "V", vc(cnt(i) * (1 if ps else 2)), lambda: vec.tensor_tensor(out=ap(o), in0=ap(i), in1=ap(j), op=op),
             [reg(i), reg(j)], [reg(o)])

    def act(o, i, func=F.Identity, bias=None, scale=None):
        def fn():
            kw = {}
            if bias is not None:
                kw["bias"] = sv(bias)
            if scale is not None:
                kw["scale"] = sv(scale)
            return sca.activation(out=ap(o), in_=ap(i), func=func, **kw)
        _add(gr, "S", FIX["S"] + cnt(i) * CY, fn, [reg(i)] + scal(bias) + scal(scale), [reg(o)])

    def mm(lst):
        def fn():
            x = None
            for o, l, r, s, e in lst:
                x = ten.matmul(ap(o), ap(l), ap(r), s, e)
            return x
        c = FIX["P"]; R = []; Wr = []
        for o, l, r, s, e in lst:
            c += max(min(64, cnt(l)), cnt(r)) * CY * (4 if BUF[l[0]][2] == "float32" else 1)
            R += [reg(l), reg(r)]; Wr.append(reg(o))
        lo = min(x[1] for x in Wr); hi = max(x[2] for x in Wr)
        _add(gr, "P", c, fn, sorted(set(R)), [(Wr[0][0], lo, hi)])

    dn = [0]

    def load(q, o, src):
        s = "d%d" % dn[0]; dn[0] += 1
        eng = {"Y": syn, "S": sca}[q]
        byts = cnt(o) * 128 * 2
        _add(gr, q, 2.0 + byts / 150000.0, lambda: eng.dma_start(ap(o), src), [], [reg(o)], sem=s)

    def store(q, dst, i):
        s = "d%d" % dn[0]; dn[0] += 1
        eng = {"Y": syn, "S": sca}[q]
        _add(gr, q, 2.0 + cnt(i) * 256 / 150000.0, lambda: eng.dma_start(dst, ap(i)), [reg(i)], [], sem=s)

    load("Y", full("vein0"), T.vein[:]); load("S", full("front0"), T.front[:])
    load("Y", full("w0"), T.w[:]); load("S", full("lim0"), T.lim[:])
    for k in range(4):
        load("YS"[k & 1], ("X", k * 1024, (k + 1) * 1024), T.rock[:, k * 1024:(k + 1) * 1024])

    def iota(name, pattern, base, cm, cols):
        _add(gr, "G", 0.15 + 2 * cols * CY, lambda: g.iota(sl(name), pattern, base, cm), [], [full(name)])

    iota("PI", [[1, 1]], 0, 1, 1); iota("CI", [[1, 128]], 0, 0, 128); iota("WC", [[1, 160]], -16, 0, 160)
    iota("TRI0", [[16, 16]], TRASH, 0, 16)
    iota("REPI", [[1, 128], [0, 16]], 0, 0, 2048)
    nc = [0]

    def col():
        nc[0] += 1
        return ("cf", nc[0] - 1, nc[0])
    ni = [0]

    def icol():
        ni[0] += 1
        return ("ci", ni[0] - 1, ni[0])
    PI, CI, C15, CG = full("PI"), full("CI"), full("C15"), full("CG")
    PF = col(); tc(PF, PI)
    k_i, g_i = icol(), icol()
    ts(k_i, PI, 15, A.bitwise_and); ts(g_i, PI, 4, A.arith_shift_right)
    KF, GF = col(), col(); tc(KF, k_i); tc(GF, g_i)
    ts(CG, CI, 4, A.arith_shift_right); ts(C15, CI, 15, A.bitwise_and)
    BDb, BDh, Ib, NIb, NIh = full("BDb"), full("BDh"), full("Ib"), full("NIb"), full("NIh")
    ts(BDb, CG, GF, A.is_equal); tc(BDh, BDb)
    ts(Ib, CI, PF, A.is_equal); ts(NIb, Ib, -1.0, A.mult)
    ts(full("WI"), full("WC"), PF, A.is_equal); Ih = ("WI", 16, 144)
    ts(NIh, Ih, -1.0, A.mult)
    WF, LF = col(), col(); tc(WF, full("w0")); tc(LF, full("lim0"))
    W2, S256 = full("W2"), full("S256")
    ts(W2, BDb, WF, A.mult, 2.0, A.mult); ts(S256, BDb, 256.0, A.mult)
    KS = col(); ts(KS, KF, 256.0, A.mult, 1.0, A.add)
    NKC = []
    for m in range(3):
        c = col(); NKC.append(c); sc = float(1 << (5 + m))
        ts(c, KF, 37.0 * sc, A.mult, (613 * m + 2048) * sc - 8388608.0, A.add)
    TOP = full("TOP"); tc(TOP, LF)
    ts(full("REP"), full("REPI"), PF, A.is_equal)
    IND, IND128 = full("IND"), full("IND128")
    ts(IND, ("CI", 0, 8), GF, A.is_equal); ts(IND128, IND, 128.0, A.mult)
    OHK = full("OHK"); ts(OHK, ("CI", 0, 16), KF, A.is_equal)

    def BL(l):
        return ("BL", l * 128, l * 128 + 128)

    def PW(j):
        return ("PW", j * 128, j * 128 + 128)
    for l in range(16):
        ts(BL(l), BDh, ("OHK", l, l + 1), A.mult)
    for j in range(8):
        ts(PW(j), Ib, float(1 << j), A.mult)
    LT, LT0 = full("LT"), full("LT0")
    ts(LT0, C15, KF, A.is_gt, 4.0, A.mult); tt(LT0, LT0, BDb, A.mult); tt(LT, LT0, Ib, A.subtract)
    BD0 = full("BD0"); ts(BD0, BDb, ("OHK", 0, 1), A.mult)
    KBD, BD64 = full("KBD"), full("BD64")
    ts(KBD, BDb, KF, A.mult, 64.0, A.mult); ts(BD64, BDb, 64.0, A.mult)
    HC = full("HC"); ts(HC, ("CI", 0, 64), 0.0625, A.mult)
    P16, P15c = col(), col()
    ts(P16, KF, 0.0, A.mult, 65536.0, A.add)
    for b in range(4):
        x, y = icol(), col()
        ts(x, k_i, b, A.arith_shift_right, 1, A.bitwise_and)
        ts(y, x, 2.0 ** -(1 << b) - 1.0, A.mult, 1.0, A.add)
        tt(P16, P16, y, A.mult)
    ts(P15c, P16, 0.5, A.mult)
    M2C = col(); ts(M2C, KF, -64.0, A.mult, 64.0 * 31 + 63, A.add)
    RB = full("RB"); ts(RB, ("C15", 0, 64), KF, A.is_equal)
    SC0 = full("SC0"); ts(SC0, ("C15", 0, 64), 0.0, A.not_equal)
    for c in range(8):
        _add(gr, "V", vc(16), lambda c=c: vec.tensor_scalar(out=T.TRI[:, c, :], in0=sl("C15", 0, 16), scalar1=ap(KF), scalar2=None, op0=A.is_gt),
             [("C15", 0, 16), KF], [("TRI", c, c + 1)])
    ts(full("TRC"), full("TRI0"), KF, A.add)
    _add(gr, "V", vc(128), lambda: vec.memset(sl("ONE"), 1.0), [], [full("ONE")])
    for k in range(2):
        _add(gr, "V", vc(2048), lambda k=k: vec.memset(sl("TAB%d" % k), 0.0), [], [full("TAB%d" % k)])

    def RM(s):
        return ("RM", s * 128, s * 128 + 128)

    def CC(s):
        return ("CC", s * 8, s * 8 + 8)

    def PM(s):
        return ("PM", (s - 1) * 128, s * 128)
    rot_i = icol(); rot_h = icol(); lo_i = icol()
    for s in (0, 1, 6, 2, 5, 3, 4):
        rf, lf, hf = col(), col(), col()
        if s == 0:
            ts(rot_i, PI, 0.0, A.add)
        else:
            ts(rot_i, PI, float(1 << s), A.mult); ts(rot_i, rot_i, 127, A.bitwise_and)
            ts(rot_h, PI, 7 - s, A.arith_shift_right); tt(rot_i, rot_i, rot_h, A.add)
        tc(rf, rot_i); ts(lo_i, rot_i, 15, A.bitwise_and); tc(lf, lo_i)
        ts(lo_i, rot_i, 4, A.arith_shift_right); tc(hf, lo_i)
        ts(RM(s), C15, lf, A.is_equal); ts(CC(s), ("CI", 0, 8), hf, A.is_equal)
        if 1 <= s <= 5:
            ts(PM(s), CI, rf, A.is_equal)

    for k in range(2):
        for p in range(2):
            ts(("TB0%d" % k, 384 + 64 * p, 448 + 64 * p), ("front0", k * H + p, (k + 1) * H, 2), -2048.0, A.add)
            act(("Z0%d" % k, 64 * p, 64 * p + 64), ("vein0", k * H + p, (k + 1) * H, 2))

    def view(h, t):
        s = str(h)
        return lambda n, a=None, b=None, st=None: ((n + s,) + ((0, BUF[n + s][1][1]) if a is None else ((a, b) if st is None else (a, b, st))))

    BU, BM, BS0, BS1 = "B6", "B7", "B4", "B5"
    BK = ["B2", "B3"]

    def numbers(h, t):
        v = view(h, t)
        Z = full("Z%d%d" % (t, h)); tb = "TB%d%d" % (t, h); NCt = (tb, 384, 512)
        mm([((BU, 256, 384), Ih, NCt, True, True)])
        act((BU, 384, 512), (BU, 256, 384), bias=None, scale=None) if False else None
        for m in range(3):
            act(v("NK", m * H, m * H + H), (BU, 256, 384), F.Identity, NKC[m], float(1 << (5 + m)))
        mm([((BU, 0, 128), W2, Z, True, True), ((BU, 128, 256), S256, Z, True, True)])
        ts(v("VI"), (BU, 0, 256), 1.0, A.add); ts(v("VS"), v("VI"), 4095, A.bitwise_and)
        ts((BU, 384, 512), (BU, 256, 384), 2048.0, A.add)
        tt((BU, 0, 128), (BU, 384, 512), v("VS", 0, 128), A.mult)
        for m in range(3):
            o = (m * H, m * H + H)
            tt(v("QI", *o), (BU, 0, 128), v("NK", *o), A.add)
            ts(v("QS", *o), v("QI", *o), 5 + m, A.arith_shift_right, 4095, A.bitwise_and)
            tc(v("OF", *o), v("QS", *o))
        bk = "B%d" % (dbank[0] & 1); dbank[0] += 1
        mm([((bk, 0, 128), Z, Ib, True, True)])
        act(v("ZT"), (bk, 0, 128)); act(v("NZT"), (bk, 0, 128), scale=-1.0)
        for a in range(0, 16 * max(VPART), 512):
            bk = "B%d" % (dbank[0] & 1); dbank[0] += 1
            mm([((bk, 0, 512), v("ZT"), ("REP", a, a + 512), True, True)])
            act(v("ZR", a, a + 512), (bk, 0, 512))
        ts((tb, 0, 384), v("OF"), -2048.0, A.add)
        ts(v("MS"), v("VS", 128, 256), KS, A.is_equal)
        ts(v("U32"), v("VS", 64, 128), 16.0, A.mult, -16.0 - 8388608.0, A.add)
        ts(v("ZQ"), Z, 0.25, A.mult, 1031.625, A.add)

    unit = [0]
    dbank = [0]

    def scores(h, t):
        v = view(h, t); zr = "ZR%d" % h
        for m in range(3):
            u = unit[0] % 3; unit[0] += 1
            D, G, L = "D%d" % u, "G%d" % u, "L%d" % u
            nv = VPART[m]
            of = "OF%d" % h
            XW = ("X", 0, W)

            def vg(a, b, m=m, D=D):
                _add(gr, "V", 0.05 + 1.5 * CY * 16 * (b - a), lambda: vec.tensor_tensor(
                    out=sl(D, 16 * a, 16 * b), in0=sl("X", 0, W).indirect(sl(of, m * H + a, m * H + b)), in1=sl(zr, 16 * a, 16 * b), op=A.subtract),
                    [XW, (of, m * H + a, m * H + b), (zr, 16 * a, 16 * b)], [(D, 16 * a, 16 * b)])

            def sg(a, b, m=m, G=G):
                _add(gr, "S", 0.065 + 1.5 * CY * 16 * (b - a), lambda: sca.activation(
                    out=sl(G, 16 * a, 16 * b), in_=sl("X", 0, W).indirect(sl(of, m * H + a, m * H + b)), func=F.Identity),
                    [XW, (of, m * H + a, m * H + b)], [(G, 16 * a, 16 * b)])
            for a in range(0, nv, 32):
                vg(a, a + 32)
            for a in range(nv, H, 32):
                sg(a, a + 32)
            for a in range(nv, H, 32):
                bk = "B%d" % (dbank[0] & 1); dbank[0] += 1

                r = (16 * a, 16 * a + 512)
                mm([((bk, 0, 512), v("NZT"), ("REP",) + r, True, False), ((bk, 0, 512), Ib, (G,) + r, False, True)])
                act((D, 16 * a, 16 * a + 512), (bk, 0, 512), F.Abs)
            for a in range(0, nv, 32):
                act((D, 16 * a, 16 * a + 512), (D, 16 * a, 16 * a + 512), F.Abs)
            for a in range(0, H, 64):
                r = (16 * a, 16 * a + 1024)
                ts((L,) + r, (D,) + r, TOP, A.is_le, 2.0 * m + 0.4375, A.add)
            for k0 in range(0, 16, 8):
                mm([x for k in range(k0, k0 + 8) for x in (
                    ((BK[h], m * H + k, m * H + 128, 16), (D, k, 2048, 16), IND128, True, False),
                    ((BK[h], m * H + k, m * H + 128, 16), (L, k, 2048, 16), IND, False, True))])

    def choose(h, t):
        v = view(h, t); B = BK[h]; tb = "TB%d%d" % (t, h)
        act(v("K0"), (B, 0, 128))
        tt(v("K1"), v("K0"), (B, 128, 256), A.min)
        tt(v("KI"), v("K1"), (B, 256, 384), A.min)
        ts(v("YI"), v("KI"), 4, A.arith_shift_right, 7, A.bitwise_and)
        ts(v("OK"), v("KI"), 16, A.bitwise_and)
        for m in range(3):
            ts(v("MK", m * H, m * H + H), v("YI"), 2.0 * m + 1.0, A.is_equal)
        ts(v("MK", 384, 512), v("OK"), 0.0, A.is_equal)
        mm([((BS0, s * H, s * H + H), v("MK", s * H, s * H + H), Ib, True, True) for s in range(4)])
        tt(v("PR"), (BS0, 0, 512), full(tb), A.mult)
        mm([((BM, 0, 128), Ih, v("PR", s * H, s * H + H), s == 0, s == 3) for s in range(4)])

    def meet(h, t):
        v = view(h, t)
        NPs, NPj, NPa = (BM, 0, 64), (BM, 64, 128), (BM, 0, 128)
        ts(v("GS"), NPs, 0.125, A.mult, 1287.5625, A.add)
        ts(v("JR", 0, 64), NPj, 0.125, A.mult, 1287.5625, A.add)
        tc(v("FC"), NPa)
        act(v("NF"), NPa, F.Identity, B2048)
        act(v("J32"), NPj, F.Identity, B65536, 32.0)
        tc(v("JR", 64, 128), v("JR", 0, 64)); tc(v("JR", 128, 256), v("JR", 0, 128))
        for x in range(2):
            bk = (BS0, BS1)[x]
            mm([((bk, 64 * l, 64 * l + 64), BL(8 * x + l), v("GS"), True, True) for l in range(8)])
            for y in range(2):
                tt(v("EQ", 512 * x + 256 * y, 512 * x + 256 * y + 256), (bk, 256 * y, 256 * y + 256), v("JR"), A.is_equal)
        for x in range(4):
            lo, hi = max(2, 8 * x), min(31, 8 * x + 8)
            bk = (BS0, BS1)[x & 1]
            mm([((bk, 64 * (d - 8 * x), 64 * (d - 8 * x) + 64), ("WI", d, d + 128), v("FC", 64, 128), True, True) for d in range(lo, hi)])
            act(v("TAB", 64 * lo, 64 * hi), (bk, 64 * (lo - 8 * x), 64 * (hi - 8 * x)))
        for x in range(2):
            mm([((BM, 128 + 64 * x, 192 + 64 * x), PW(7 - l), v("EQ", 512 * x + 64 * l, 512 * x + 64 * l + 64), l == 0, l == 7) for l in range(8)])
        ts(v("M12"), (BM, 128, 256), 0.0, A.is_gt)
        mm([((BM, 256, 320), LT, v("M12", 0, 64), True, False), ((BM, 256, 320), LT, v("M12", 64, 128), False, True)])
        ts(v("OH"), (BM, 256, 320), 0.0, A.is_lt)
        tt(v("P12", 0, 64), (BM, 128, 192), v("OH"), A.mult)
        tt(v("P12", 64, 128), (BM, 192, 256), v("OH"), A.mult)
        mm([((BM, 320, 384), S256, v("P12", 0, 64), True, False), ((BM, 320, 384), BDb, v("P12", 64, 128), False, True)])
        ts(v("TP"), (BM, 320, 384), P15c, A.is_ge)
        mm([((BM, 384, 448), KBD, v("OH"), True, False), ((BM, 384, 448), BDb, HC, False, False), ((BM, 384, 448), BD64, v("TP"), False, True)])
        tt(v("DM"), (BM, 384, 448), RB, A.mult)
        _add(gr, "V", vc(64), lambda: vec.tensor_tensor_scan(ap(v("DS")), ap(SC0), ap(v("DM")), 0.0, A.mult, A.add), [SC0, v("DM")], [v("DS")])
        tc(v("DO"), v("DS", 15, 64, 16))
        do = "DO%d" % h; tab = "TAB%d" % h; new = "NEW%d" % h
        _add(gr, "S", 0.065 + 64 * 1.5 * CY, lambda: sca.activation(out=sl(new, 0, 64), in_=sl(tab).indirect(sl(do)), func=F.Identity),
             [full(tab), full(do)], [(new, 0, 64)])
        ts(v("MS1"), (BM, 320, 384), P16, A.is_ge)
        ts(v("MS2"), (BM, 384, 448), M2C, A.is_le)
        tt(v("MM", 0, 64), v("MS1"), v("MS2"), A.mult)
        ts(v("MM", 64, 128), (BM, 256, 320), 0.0, A.not_equal)
        tt((BM, 448, 512), v("NF", 64, 128), v("NF", 0, 64), A.mult)
        tt((BM, 448, 512), (BM, 448, 512), v("U32"), A.add)
        tt(v("JQ"), (BM, 448, 512), v("J32"), A.add)
        ts(v("JT"), v("JQ"), 5, A.arith_shift_right, 4095, A.bitwise_and)
        ts(v("NEW", 64, 128), v("JT"), -2048.0, A.add)
        tt(v("PB"), v("MM"), v("FC"), A.mult)
        tt(v("PA", 64, 128), v("NEW", 64, 128), v("MM", 64, 128), A.mult)
        tt(v("PA", 0, 64), v("NEW", 0, 64), v("MM", 0, 64), A.mult)
        F2 = (BK[h], 0, 128)
        mm([(F2, Ih, v("FC"), True, False), (F2, NIh, v("PB"), False, False), (F2, Ih, v("PA"), False, True)])
        if t < V - 1:
            _add(gr, "V", vc(64), lambda: vec.tensor_reduce(out=ap(v("CNT")), in_=ap(v("OH")), axis=AxisListType.X, op=A.add), [v("OH")], [v("CNT")])

    def send(name, h, t):
        src = full("S%s%d%d" % (name, t, h))
        dst = full("Z%d%d" % (t + 1, h)) if name == "Z" else ("TB%d%d" % (t + 1, h), 384, 512)
        rid, pid, _ = topo.addr(nxt)
        en = topo.engines(core, nxt)
        en = en[:len(en) // 2] if name == "N" else en[len(en) // 2:]
        msk = sum(1 << e for e in en)
        rs = "a%s%d%d" % (name.lower(), t + 1, h)
        NE.append(len(en))
        x = ("link", 8 * len(NE), 8 * len(NE) + 1)
        _add(gr, "G", 0.5, lambda: g.remote_dma(ap(dst), ap(src), T.sem[rs], T.sem.loc, pid, rid, msk), [src], [x], sem="loc")
        _add(gr, "A", 2.5, None, [x], [dst], sem=(rs, len(en)))

    NE = []

    def mine(h, t):
        v = view(h, t); B = BK[h]; s = t + 1
        F2, ET, EB, ELp, ELn, DW = (B, 0, 128), (B, 128, 256), (B, 256, 384), (B, 384, 392), (B, 392, 400), (B, 400, 408)
        Z = full("Z%d%d" % (t, h))
        tt(v("FS"), F2, v("MS"), A.mult)
        mm([(ET, v("FS"), BDh, True, True)])
        tt(v("EMP"), ET, RM(0), A.mult)
        mm([(ELp, v("EMP"), CC(0), True, True)])
        if t < V - 1:
            for p in range(2):
                tc(("SN%d%d" % (t, h), 64 * p, 64 * p + 64), (B, p, 128, 2))
            send("N", h, t)
        else:
            for q in range(4):
                act(("YF", h * H + 32 * q, h * H + 32 * q + 32), (B, q, 128, 4), F.Identity, B2048)
        ts(v("YO"), ELp, 2048.0, A.add)
        yo = "YO%d" % h; yb = "YB%d" % h
        _add(gr, "S", 0.065 + 128 * 1.5 * CY, lambda: sca.activation(out=sl(yb), in_=sl("X", 0, W).indirect(sl(yo)), func=F.Identity),
             [("X", 0, W), full(yo)], [full(yb)])
        tt(v("EMN"), ET, RM(s), A.mult); tc(v("ETF"), ET); ts(v("EPF"), ELp, 2048.0, A.add)
        mm([(ELn, v("EMN"), CC(s), True, True), (EB, v("ETF"), PM(s), True, True)])
        tc(v("ECL"), ELn); tc(v("EC"), EB)
        mm([((B, 0, 128), Ib, v("YB"), True, False), ((B, 0, 128), Ib, Z, False, True),
            ((B, 128, 256), Ib, v("YB"), True, False), ((B, 128, 256), NIh, v("ZQ"), False, True)])
        ts(v("ZH"), (B, 0, 128), 0.5, A.mult, 1031.75, A.add)
        if t < V - 1:
            for p in range(2):
                ts(("SZ%d%d" % (t, h), 64 * p, 64 * p + 64), v("ZH", p, 128, 2), -1032.0, A.add)
            send("Z", h, t)
        else:
            for q in range(4):
                ts(("YZ", h * H + 32 * q, h * H + 32 * q + 32), v("ZH", q, 128, 4), -1032.0, A.add)
        act(v("NX"), (B, 128, 256), F.Relu, B1032)
        ed = "ED%d" % h; ec = "EC%d" % h
        for c in range(8):
            _add(gr, "V", vc(64), lambda c=c: vec.tensor_scalar(out=T[ed][:, c, 0:H - 16 * c], in0=sl(ec, 16 * c, H),
                 scalar1=ap(v("ECL", c, c + 1)), scalar2=None, op0=A.is_equal), [full(ec), v("ECL", c, c + 1)], [(ed, c, c + 1)])
        if h == 1:
            for c in range(8):
                _add(gr, "V", vc(64), lambda c=c: vec.tensor_scalar(out=T.EX[:, c, :], in0=sl(ec),
                     scalar1=ap(("ECL0", c, c + 1)), scalar2=None, op0=A.is_equal), [full(ec), ("ECL0", c, c + 1)], [("EX", c, c + 1)])
        _add(gr, "V", vc(256), lambda: vec.tensor_tensor(out=T[ed][:, :, 0:16], in0=T[ed][:, :, 0:16], in1=T.TRI[:], op=A.mult),
             [(ed, 0, 8), ("TRI", 0, 8)], [(ed, 0, 8)])

        def dup():
            for c in range(8):
                x = ten.matmul(T[B][:, 256 + 16 * c:384], ap(BDb), T[ed][:, c, 0:H - 16 * c], c == 0, c == 7 and h == 0)
            if h == 1:
                for c in range(8):
                    x = ten.matmul(T[B][:, 256:384], ap(BDb), T.EX[:, c, :], False, c == 7)
            return x
        _add(gr, "P", FIX["P"] + (700 + 1024 * h) * CY, dup, [reg(BDb), (ed, 0, 8)] + ([("EX", 0, 8)] if h else []), [EB])
        ts(v("FLG"), EB, 0.0, A.is_gt)
        mm([((B, 0, 128), v("FLG"), BD0, True, True)])
        tt(v("DTM"), (B, 0, 128), RM(7 - s), A.mult)
        mm([(DW, v("DTM"), CC(7 - s), True, True)])
        tt(v("T1"), DW, ("TRC", 8 * h, 8 * h + 8), A.mult)
        tt(v("T2"), v("T1"), v("EPF"), A.max)
        tc(v("SO"), v("T2"))

    def carve(h, t):
        so = "SO%d" % h; nx = "NX%d" % h
        _add(gr, "V", 0.05 + 128 * 3.5 * CY, lambda: vec.tensor_copy(out=sl("X").indirect(sl(so)), in_=sl(nx)),
             [full(so), full(nx)], [("X", 0, W + C)])

    def limits():
        B = BK[1]
        mm([((B, 408, 409), full("ONE"), full("CNT0"), True, False), ((B, 408, 409), full("ONE"), full("CNT1"), False, True)])
        tc(("EI", 0, 1), (B, 408, 409)); ts(("EI", 1, 2), ("EI", 0, 1), 3, A.bitwise_and)
        tt(TOP, ("EI", 1, 2), LF, A.add)

    B2048, B65536, B1032 = col(), col(), col()
    for c, x in ((B2048, 2048.0), (B65536, 65536.0), (B1032, 1032.0)):
        ts(c, KF, 0.0, A.mult, x, A.add)

    numbers(0, 0); numbers(1, 0)
    for t in range(V):
        scores(0, t); choose(0, t)
        scores(1, t)
        meet(0, t); mine(0, t)
        choose(1, t); meet(1, t); mine(1, t)
        if t < V - 1:
            limits()
        carve(0, t); carve(1, t)
        if t < V - 1:
            numbers(0, t + 1); numbers(1, t + 1)
    store("Y", T.yf[:], full("YF")); store("S", T.yz[:], full("YZ"))
    for k in range(4):
        store("YS"[k & 1], T.yx[:, k * 1024:(k + 1) * 1024], ("X", k * 1024, (k + 1) * 1024))

    ops = gr["ops"]
    seq = _order(ops)
    eng = {"V": vec, "S": sca, "P": ten, "G": g, "Y": syn}
    cs = {"V": "cV", "S": "cS", "P": "cP", "G": "cG"}
    count = {q: 0 for q in eng}
    seen = {q: {} for q in eng}
    for c in seq:
        o = ops[c]; q = o["q"]
        if q == "A":
            o["key"] = o["sem"]
            d = ops[o["deps"][0]] if o["deps"] else None
            o["vc"] = {}
            continue
        S = seen[q]
        want = {}
        for d in o["deps"]:
            k = ops[d].get("key")
            if k is None:
                continue
            if S.get(k[0], 0) < k[1]:
                want.setdefault(k[0], (0, None))
                if want[k[0]][0] < k[1]:
                    want[k[0]] = (k[1], d)
        for nm, (val, d) in sorted(want.items(), key=lambda kv: -ops[kv[1][1]].get("fin", 0)):
            if S.get(nm, 0) >= val:
                continue
            eng[q].wait_ge(T.sem[nm], val)
            S[nm] = max(S.get(nm, 0), val)
            for n2, v2 in ops[d]["vc"].items():
                S[n2] = max(S.get(n2, 0), v2)
        x = o["fn"]()
        o["vc"] = dict(S)
        if o["sem"] is None:
            count[q] += 1
            x.then_inc(T.sem[cs[q]], 1)
            o["key"] = (cs[q], count[q])
        elif o["sem"] == "loc":
            pass
        else:
            x.then_inc(T.sem[o["sem"]], 16)
            o["key"] = (o["sem"], 16)
    for q in "VSPG":
        if count[q]:
            g.wait_ge(T.sem[cs[q]], count[q])
    for k in range(dn[0]):
        g.wait_ge(T.sem["d%d" % k], 16)
    if NE:
        g.wait_ge(T.sem.loc, sum(NE))
    return ops
